import numpy as np
import ml_dtypes


def mxq(x, axis, fmt="e4m3"):
    dtype, down = {"e4m3": (ml_dtypes.float8_e4m3fn, 7), "e5m2": (ml_dtypes.float8_e5m2, 14)}[fmt]
    v = np.moveaxis(np.asarray(x, np.float32).astype(ml_dtypes.bfloat16).astype(np.float64), axis, -1)
    blocks = v.reshape(v.shape[:-1] + (-1, 32))
    amax = np.abs(blocks).max(-1, keepdims=True)
    byte = np.maximum(np.where(amax > 0, np.frexp(amax)[1] - 1 + 127, 0) - down, 1)
    scale = np.exp2(byte - 127.0)
    codes = (blocks / scale).astype(np.float32).astype(dtype).astype(np.float64)
    return np.moveaxis((codes * scale).reshape(v.shape), -1, axis)


WIDE = False


def mx_kscale(k):
    if not WIDE:
        return np.ones(k)
    levels = np.array([30, -30])
    if k % 512:
        return np.exp2(np.random.permutation(np.resize(levels, k // 32))).repeat(32)
    a = np.empty((k // 512, 16))
    for p in range(k // 512):
        a[p, :8] = np.random.permutation(np.resize(levels, 8))
        for g in range(8):
            far = levels[np.abs(levels - a[p, g]) >= 10]
            a[p, g + 8] = far[np.random.randint(len(far))]
    return np.exp2(a.ravel()).repeat(32)


def f64(x):
    return np.asarray(x).astype(np.float64)


def striped(idx):
    return np.tile(np.asarray(idx).reshape(-1, 16).T, (8, 1)).astype(np.uint16)


def unstriped(offs):
    return offs[:16].T.reshape(-1).astype(np.int64)


def bf(x):
    return np.asarray(x, np.float32).astype(ml_dtypes.bfloat16)


def planes(Y):
    r, m = Y.shape
    b = f64(bf(Y)).reshape(r // 32, 32, m)
    amax = np.abs(b).max(1)
    byte = np.clip(np.where(amax > 0, np.frexp(amax)[1] - 1 + 127 - 7, 1), 1, 254)
    codes = (b * np.exp2(127.0 - byte)[:, None, :]).reshape(r, m).astype(np.float32).astype(ml_dtypes.float8_e4m3fn).view(np.uint8)
    words = codes.reshape(r // 512, 128, 4, m).transpose(0, 1, 3, 2)
    return np.ascontiguousarray(words), np.ascontiguousarray(byte.astype(np.uint8).reshape(r // 512, 16, m))


K, J, N, T, B, V = 512, 512, 256, 1024, 64, 1024


def setup_inputs():
    n = np.random.standard_normal
    idx = np.random.permutation(T)[:J]
    idx2 = np.random.permutation(V)[:J]
    fj = mx_kscale(J)
    return {
        "xf": (n((K, T))).astype(np.float32),
        "ra": (np.random.uniform(0.5, 1.5, (1, J)) * fj).astype(np.float32),
        "gt": (n((N, V)) * np.exp(0.5 * n((1, V)))).astype(np.float32),
        "rb": (np.random.uniform(0.5, 1.5, (1, J)) / fj).astype(np.float32),
        "pr": (n((N, J))).astype(np.float32),
        "mom": (1.0 * n((K, N))).astype(np.float32),
        "old": (1.0 * n((K, N))).astype(np.float32),
        "offs": striped(idx),
        "offs2": striped(idx2),
    }


def reference(xf, ra, gt, rb, pr, mom, old, offs, offs2):
    idx = unstriped(offs)
    idx2 = unstriped(offs2)
    xg = f64(xf)[:, idx]
    g1 = xg.reshape(K, B, J // B).mean(axis=2)
    g2 = np.repeat(g1, J // B, axis=1)
    us = (xg - g2) * f64(ra)
    uj = us.T
    gs = (f64(gt)[:, idx2] - f64(pr)) * f64(rb)
    gj = gs.T
    ujq = mxq(uj, 0, "e5m2")
    gjq = mxq(gj, 0, "e5m2")
    w = ujq.T @ gjq
    u2 = 0.04 * w + 0.6 * f64(mom)
    y = f64(old) * 0.5 - u2 / (1.0 + np.abs(u2))
    words, scales = planes(y)
    return y, words, scales

@@ -1,0 +1,160 @@
+from contextlib import ExitStack
+
+import concourse.mybir as mybir
+from concourse.masks import make_identity
+
+K, J, N, T, V = 512, 512, 256, 1024, 1024
+FLOPS = 2 * K * J * N
+
+F32 = mybir.dt.float32
+BF16 = mybir.dt.bfloat16
+U32 = mybir.dt.uint32
+I32 = mybir.dt.int32
+U16 = mybir.dt.uint16
+U8 = mybir.dt.uint8
+E5M2 = mybir.dt.float8_e5m2_x4
+E4M3 = mybir.dt.float8_e4m3fn_x4
+ALU = mybir.AluOpType
+ACT = mybir.ActivationFunctionType
+
+P = 128
+PACK = 4
+GROUP = 8
+HALVES = N // P
+CHUNK = 64
+
+
+def tile_list_moment_centred_errors_momentum_pl_kernel(tc, xf, ra, gt, rb, pr, mom, old, offs, offs2, out_0, out_1, out_2):
+    nc = tc.nc
+    with ExitStack() as ctx:
+        keep = ctx.enter_context(tc.tile_pool(name="keep", bufs=1))
+        psum = ctx.enter_context(tc.psum_pool(name="psum", bufs=1))
+
+        x_list = keep.tile([P, J // 16], U16, name="x_list")
+        g_list = keep.tile([P, J // 16], U16, name="g_list")
+        x_rows = [keep.tile([P, T], F32, name="x_rows%d" % t) for t in range(PACK)]
+        g_rows = [keep.tile([P, V], F32, name="g_rows%d" % h) for h in range(HALVES)]
+        pr_rows = keep.tile([P, HALVES, J], F32, name="pr_rows")
+        mom_rows = keep.tile([P, PACK, N], F32, name="mom_rows")
+        old_rows = keep.tile([P, PACK, N], F32, name="old_rows")
+        ra_col = keep.tile([P, PACK], F32, name="ra_col")
+        rb_col = keep.tile([P, PACK], F32, name="rb_col", tag="rb_then_step")
+
+        xf_dealt = xf.rearrange("(p t) c -> p t c", t=PACK)
+        nc.sync.dma_start(out=x_rows[0][:], in_=xf_dealt[:, 0, :])
+        nc.sync.dma_start(x_list[:], offs)
+        nc.sync.dma_start(out=pr_rows[:], in_=pr.rearrange("(h p) j -> p h j", p=P))
+        nc.gpsimd.dma_start(out=ra_col[:], in_=ra.rearrange("o (p t) -> (o p) t", t=PACK))
+        nc.gpsimd.dma_start(out=rb_col[:], in_=rb.rearrange("o (p t) -> (o p) t", t=PACK))
+        for t in range(1, PACK):
+            nc.sync.dma_start(out=x_rows[t][:], in_=xf_dealt[:, t, :])
+        nc.sync.dma_start(g_list[:], offs2)
+        for h in range(HALVES):
+            nc.sync.dma_start(out=g_rows[h][:], in_=gt[h * P:(h + 1) * P, :])
+        nc.sync.dma_start(out=mom_rows[:], in_=mom.rearrange("(p t) n -> p t n", t=PACK))
+        nc.sync.dma_start(out=old_rows[:], in_=old.rearrange("(p t) n -> p t n", t=PACK))
+
+        ident = keep.tile([P, P], F32, name="ident")
+        make_identity(nc, ident[:])
+
+        u_codes = keep.tile([P, K], U32, name="u_codes", align_bytes=64)
+        u_scales = keep.tile([P, K], U8, name="u_scales", align_bytes=64)
+        g_codes = keep.tile([P, N], U32, name="g_codes", align_bytes=64)
+        g_scales = keep.tile([P, N], U8, name="g_scales", align_bytes=64)
+        y_codes = keep.tile([P, N], U32, name="y_codes", align_bytes=64)
+        y_scales = keep.tile([P, N], U8, name="y_scales", align_bytes=64)
+
+        def turn(bank, sources, first):
+            for i in range(PACK):
+                nc.tensor.matmul(bank[:, i, :], lhsT=sources[i], rhs=ident[:], is_transpose=True,
+                                 start=(first and i == 0), stop=(not first and i == PACK - 1))
+
+        def by_byte(picked):
+            view = picked[:].rearrange("p (q i) -> p i q", i=PACK)
+            return [view[:, i, :] for i in range(PACK)]
+
+        def weigh_and_quantise(name, bank, weights, codes, scales):
+            rounded = keep.tile([P, P, PACK], BF16, name=name, align_bytes=64)
+            nc.vector.tensor_tensor(out=rounded[:], in0=bank[:].rearrange("p i c -> p c i"),
+                                    in1=weights[:].unsqueeze(1).to_broadcast([P, P, PACK]), op=ALU.mult)
+            nc.vector.quantize_mx(out=codes.bitcast(E5M2), scales=scales, in_=rounded[:].rearrange("p c i -> p (c i)"))
+
+        u_rounded = keep.tile([P, K, PACK], BF16, name="u_rounded", align_bytes=64)
+
+        def features(t):
+            picked = keep.tile([P, J], F32, name="x_picked%d" % t)
+            nc.scalar.activation(picked[:], x_rows[t][:].indirect(x_list[:]), ACT.Copy)
+            sums = keep.tile([P, J // GROUP], F32, name="sums%d" % t)
+            nc.vector.tensor_reduce(out=sums[:], in_=picked[:].rearrange("p (b e) -> p b e", e=GROUP),
+                                    axis=mybir.AxisListType.X, op=ALU.add)
+            neg_mean = keep.tile([P, J // GROUP, 2], F32, name="neg_mean%d" % t)
+            nc.gpsimd.tensor_scalar(out=neg_mean[:], in0=sums[:].unsqueeze(2).to_broadcast([P, J // GROUP, 2]),
+                                    scalar1=-1.0 / GROUP, scalar2=0.0, op0=ALU.mult, op1=ALU.add)
+            bank = psum.tile([P, PACK, P], F32, name="x_turned", bufs=3)
+            turn(bank, by_byte(picked), True)
+            turn(bank, [neg_mean[:].rearrange("p b e -> p (b e)")] * PACK, False)
+            cols = slice(t * P, (t + 1) * P)
+            nc.vector.tensor_tensor(out=u_rounded[:, cols, :], in0=bank[:].rearrange("p i c -> p c i"),
+                                    in1=ra_col[:].unsqueeze(1).to_broadcast([P, P, PACK]), op=ALU.mult)
+            if t % 2 == 1:
+                both = slice((t - 1) * P, (t + 1) * P)
+                nc.vector.quantize_mx(out=u_codes[:, both].bitcast(E5M2), scales=u_scales[:, both],
+                                      in_=u_rounded[:, both, :].rearrange("p c i -> p (c i)"))
+
+        features(0)
+        g_banks = []
+        for h in range(HALVES):
+            neg_pr = keep.tile([P, PACK, P], F32, name="neg_pr%d" % h)
+            nc.gpsimd.tensor_scalar(out=neg_pr[:], in0=pr_rows[:, h, :].rearrange("p (q i) -> p i q", i=PACK),
+                                    scalar1=-1.0, scalar2=0.0, op0=ALU.mult, op1=ALU.add)
+            bank = psum.tile([P, PACK, P], F32, name="g_turned%d" % h)
+            turn(bank, [neg_pr[:, i, :] for i in range(PACK)], True)
+            g_banks.append(bank)
+        for t in range(1, PACK):
+            features(t)
+
+        y_out = out_0.rearrange("(p t) n -> p t n", t=PACK)
+        words_out = out_1.rearrange("z p c r -> (z p) (c r)").bitcast(I32)
+        for h in range(HALVES):
+            cols = slice(h * P, (h + 1) * P)
+            picked = keep.tile([P, J], F32, name="g_picked%d" % h)
+            nc.scalar.activation(picked[:], g_rows[h][:].indirect(g_list[:]), ACT.Copy)
+            turn(g_banks[h], by_byte(picked), False)
+            weigh_and_quantise("g_rounded%d" % h, g_banks[h], rb_col, g_codes[:, cols], g_scales[:, cols])
+
+        for h in range(HALVES):
+            cols = slice(h * P, (h + 1) * P)
+            moment = psum.tile([P, PACK, P], F32, name="moment%d" % h)
+            for t in range(PACK):
+                rows = slice(t * P, (t + 1) * P)
+                nc.tensor.matmul_mx(out=moment[:, t, :], lhsT=u_codes[:, rows].bitcast(E5M2), lhsT_scale=u_scales[:, rows],
+                                    rhs=g_codes[:, cols].bitcast(E5M2), rhs_scale=g_scales[:, cols], start=True, stop=True)
+            y = keep.tile([P, PACK, P], F32, name="y%d" % h)
+            for c0 in range(0, P, CHUNK):
+                n0 = h * P + c0
+                part = slice(c0, c0 + CHUNK)
+                ns = slice(n0, n0 + CHUNK)
+                step = keep.tile([P, PACK, CHUNK], F32, name="step%d" % n0, tag="rb_then_step" if n0 == 0 else "step%d" % n0)
+                nc.vector.scalar_tensor_tensor(out=step[:], in0=mom_rows[:, :, ns], scalar=15.0, in1=moment[:, :, part],
+                                               op0=ALU.mult, op1=ALU.add)
+                size = keep.tile([P, PACK, CHUNK], F32, name="size%d" % n0)
+                nc.scalar.activation(size[:], step[:], ACT.Abs)
+                root = keep.tile([P, PACK, CHUNK], F32, name="root%d" % n0)
+                nc.scalar.activation(root[:], size[:], ACT.Abs_reciprocal_sqrt, bias=25.0)
+                inverse = keep.tile([P, PACK, CHUNK], F32, name="inverse%d" % n0)
+                nc.scalar.activation(inverse[:], root[:], ACT.Square)
+                soft = keep.tile([P, PACK, CHUNK], F32, name="soft%d" % n0)
+                nc.vector.tensor_tensor(out=soft[:], in0=step[:], in1=inverse[:], op=ALU.mult)
+                nc.vector.scalar_tensor_tensor(out=y[:, :, part], in0=old_rows[:, :, ns], scalar=0.5, in1=soft[:],
+                                               op0=ALU.mult, op1=ALU.subtract)
+                y_rounded = keep.tile([P, CHUNK, PACK], BF16, name="y_rounded%d" % n0, align_bytes=64)
+                nc.scalar.copy(out=y_rounded[:], in_=y[:, :, part].rearrange("p t c -> p c t"))
+                nc.vector.quantize_mx(out=y_codes[:, ns].bitcast(E4M3), scales=y_scales[:, ns],
+                                      in_=y_rounded[:].rearrange("p c t -> p (c t)"))
+            nc.sync.dma_start(out=y_out[:, :, cols], in_=y[:])
+            nc.sync.dma_start(out=words_out[:, cols], in_=y_codes[:, cols].bitcast(I32))
+
+        scales_out = out_2.rearrange("z q c -> (z q) c").bitcast(I32)
+        for q in range(4):
+            queue = nc.sync if q % 2 == 0 else nc.scalar
+            queue.dma_start(out=scales_out[4 * q:4 * q + 4, :], in_=y_scales[32 * q:32 * q + 4, :].bitcast(I32))

@@ -54,6 +54,11 @@ def tile_list_moment_centred_errors_momentum_pl_kernel(tc, xf, ra, gt, rb, pr, m
         nc.sync.dma_start(out=mom_rows[:], in_=mom.rearrange("(p t) n -> p t n", t=PACK))
         nc.sync.dma_start(out=old_rows[:], in_=old.rearrange("(p t) n -> p t n", t=PACK))
 
+        warm_in = keep.tile([P, 1], F32, name="warm_in")
+        warm_out = keep.tile([P, 1], F32, name="warm_out")
+        nc.vector.memset(warm_in[:], 1.0)
+        nc.scalar.activation(warm_out[:], warm_in[:], ACT.Abs_reciprocal_sqrt)
+
         ident = keep.tile([P, P], F32, name="ident")
         make_identity(nc, ident[:])
 
@@ -69,14 +74,17 @@ def tile_list_moment_centred_errors_momentum_pl_kernel(tc, xf, ra, gt, rb, pr, m
                 nc.tensor.matmul(bank[:, i, :], lhsT=sources[i], rhs=ident[:], is_transpose=True,
                                  start=(first and i == 0), stop=(not first and i == PACK - 1))
 
-        def by_byte(picked):
-            view = picked[:].rearrange("p (q i) -> p i q", i=PACK)
-            return [view[:, i, :] for i in range(PACK)]
+        def by_byte(name, picked, sign):
+            dealt = keep.tile([P, PACK, P], F32, name=name)
+            nc.gpsimd.tensor_scalar(out=dealt[:], in0=picked[:].rearrange("p (q i) -> p i q", i=PACK),
+                                    scalar1=sign, scalar2=0.0, op0=ALU.mult, op1=ALU.add)
+            return [dealt[:, i, :] for i in range(PACK)]
 
         def weigh_and_quantise(name, bank, weights, codes, scales):
             rounded = keep.tile([P, P, PACK], BF16, name=name, align_bytes=64)
-            nc.vector.tensor_tensor(out=rounded[:], in0=bank[:].rearrange("p i c -> p c i"),
-                                    in1=weights[:].unsqueeze(1).to_broadcast([P, P, PACK]), op=ALU.mult)
+            nc.vector.scalar_tensor_tensor(out=rounded[:], in0=bank[:].rearrange("p i c -> p c i"), scalar=-1.0,
+                                           in1=weights[:].unsqueeze(1).to_broadcast([P, P, PACK]),
+                                           op0=ALU.mult, op1=ALU.mult)
             nc.vector.quantize_mx(out=codes.bitcast(E5M2), scales=scales, in_=rounded[:].rearrange("p c i -> p (c i)"))
 
         u_rounded = keep.tile([P, K, PACK], BF16, name="u_rounded", align_bytes=64)
@@ -84,6 +92,7 @@ def tile_list_moment_centred_errors_momentum_pl_kernel(tc, xf, ra, gt, rb, pr, m
         def features(t):
             picked = keep.tile([P, J], F32, name="x_picked%d" % t)
             nc.scalar.activation(picked[:], x_rows[t][:].indirect(x_list[:]), ACT.Copy)
+            dealt = by_byte("x_dealt%d" % t, picked, 1.0)
             sums = keep.tile([P, J // GROUP], F32, name="sums%d" % t)
             nc.vector.tensor_reduce(out=sums[:], in_=picked[:].rearrange("p (b e) -> p b e", e=GROUP),
                                     axis=mybir.AxisListType.X, op=ALU.add)
@@ -91,24 +100,22 @@ def tile_list_moment_centred_errors_momentum_pl_kernel(tc, xf, ra, gt, rb, pr, m
             nc.gpsimd.tensor_scalar(out=neg_mean[:], in0=sums[:].unsqueeze(2).to_broadcast([P, J // GROUP, 2]),
                                     scalar1=-1.0 / GROUP, scalar2=0.0, op0=ALU.mult, op1=ALU.add)
             bank = psum.tile([P, PACK, P], F32, name="x_turned", bufs=3)
-            turn(bank, by_byte(picked), True)
+            turn(bank, dealt, True)
             turn(bank, [neg_mean[:].rearrange("p b e -> p (b e)")] * PACK, False)
             cols = slice(t * P, (t + 1) * P)
             nc.vector.tensor_tensor(out=u_rounded[:, cols, :], in0=bank[:].rearrange("p i c -> p c i"),
                                     in1=ra_col[:].unsqueeze(1).to_broadcast([P, P, PACK]), op=ALU.mult)
-            if t % 2 == 1:
-                both = slice((t - 1) * P, (t + 1) * P)
+            if t % 4 == 3:
+                both = slice((t - 3) * P, (t + 1) * P)
                 nc.vector.quantize_mx(out=u_codes[:, both].bitcast(E5M2), scales=u_scales[:, both],
                                       in_=u_rounded[:, both, :].rearrange("p c i -> p (c i)"))
 
         features(0)
         g_banks = []
         for h in range(HALVES):
-            neg_pr = keep.tile([P, PACK, P], F32, name="neg_pr%d" % h)
-            nc.gpsimd.tensor_scalar(out=neg_pr[:], in0=pr_rows[:, h, :].rearrange("p (q i) -> p i q", i=PACK),
-                                    scalar1=-1.0, scalar2=0.0, op0=ALU.mult, op1=ALU.add)
             bank = psum.tile([P, PACK, P], F32, name="g_turned%d" % h)
-            turn(bank, [neg_pr[:, i, :] for i in range(PACK)], True)
+            pr_view = pr_rows[:, h, :].rearrange("p (q i) -> p i q", i=PACK)
+            turn(bank, [pr_view[:, i, :] for i in range(PACK)], True)
             g_banks.append(bank)
         for t in range(1, PACK):
             features(t)
@@ -119,7 +126,7 @@ def tile_list_moment_centred_errors_momentum_pl_kernel(tc, xf, ra, gt, rb, pr, m
             cols = slice(h * P, (h + 1) * P)
             picked = keep.tile([P, J], F32, name="g_picked%d" % h)
             nc.scalar.activation(picked[:], g_rows[h][:].indirect(g_list[:]), ACT.Copy)
-            turn(g_banks[h], by_byte(picked), False)
+            turn(g_banks[h], by_byte("g_dealt%d" % h, picked, -1.0), False)
             weigh_and_quantise("g_rounded%d" % h, g_banks[h], rb_col, g_codes[:, cols], g_scales[:, cols])
 
         for h in range(HALVES):
@@ -148,7 +155,7 @@ def tile_list_moment_centred_errors_momentum_pl_kernel(tc, xf, ra, gt, rb, pr, m
                 nc.vector.scalar_tensor_tensor(out=y[:, :, part], in0=old_rows[:, :, ns], scalar=0.5, in1=soft[:],
                                                op0=ALU.mult, op1=ALU.subtract)
                 y_rounded = keep.tile([P, CHUNK, PACK], BF16, name="y_rounded%d" % n0, align_bytes=64)
-                nc.scalar.copy(out=y_rounded[:], in_=y[:, :, part].rearrange("p t c -> p c t"))
+                (nc.scalar.copy if c0 == 0 else nc.vector.tensor_copy)(out=y_rounded[:], in_=y[:, :, part].rearrange("p t c -> p c t"))
                 nc.vector.quantize_mx(out=y_codes[:, ns].bitcast(E4M3), scales=y_scales[:, ns],
                                       in_=y_rounded[:].rearrange("p c t -> p (c t)"))
             nc.sync.dma_start(out=y_out[:, :, cols], in_=y[:])

@@ -54,11 +54,6 @@ def tile_list_moment_centred_errors_momentum_pl_kernel(tc, xf, ra, gt, rb, pr, m
         nc.sync.dma_start(out=mom_rows[:], in_=mom.rearrange("(p t) n -> p t n", t=PACK))
         nc.sync.dma_start(out=old_rows[:], in_=old.rearrange("(p t) n -> p t n", t=PACK))
 
-        warm_in = keep.tile([P, 1], F32, name="warm_in")
-        warm_out = keep.tile([P, 1], F32, name="warm_out")
-        nc.vector.memset(warm_in[:], 1.0)
-        nc.scalar.activation(warm_out[:], warm_in[:], ACT.Abs_reciprocal_sqrt)
-
         ident = keep.tile([P, P], F32, name="ident")
         make_identity(nc, ident[:])
 

@@ -22,6 +22,7 @@ PACK = 4
 GROUP = 8
 HALVES = N // P
 CHUNK = 64
+RUN = 4
 
 
 def tile_list_moment_centred_errors_momentum_pl_kernel(tc, xf, ra, gt, rb, pr, mom, old, offs, offs2, out_0, out_1, out_2):
@@ -34,25 +35,31 @@ def tile_list_moment_centred_errors_momentum_pl_kernel(tc, xf, ra, gt, rb, pr, m
         g_list = keep.tile([P, J // 16], U16, name="g_list")
         x_rows = [keep.tile([P, T], F32, name="x_rows%d" % t) for t in range(PACK)]
         g_rows = [keep.tile([P, V], F32, name="g_rows%d" % h) for h in range(HALVES)]
-        pr_rows = keep.tile([P, HALVES, J], F32, name="pr_rows")
+        pr_rows = [keep.tile([P, J], F32, name="pr_rows%d" % h) for h in range(HALVES)]
         mom_rows = keep.tile([P, PACK, N], F32, name="mom_rows")
         old_rows = keep.tile([P, PACK, N], F32, name="old_rows")
         ra_col = keep.tile([P, PACK], F32, name="ra_col")
         rb_col = keep.tile([P, PACK], F32, name="rb_col", tag="rb_then_step")
+        nc.scalar.dma_start(out=ra_col[:], in_=ra.rearrange("o (p t) -> (o p) t", t=PACK))
+        nc.scalar.dma_start(out=rb_col[:], in_=rb.rearrange("o (p t) -> (o p) t", t=PACK))
 
         xf_dealt = xf.rearrange("(p t) c -> p t c", t=PACK)
         nc.sync.dma_start(out=x_rows[0][:], in_=xf_dealt[:, 0, :])
         nc.sync.dma_start(x_list[:], offs)
-        nc.sync.dma_start(out=pr_rows[:], in_=pr.rearrange("(h p) j -> p h j", p=P))
-        nc.gpsimd.dma_start(out=ra_col[:], in_=ra.rearrange("o (p t) -> (o p) t", t=PACK))
-        nc.gpsimd.dma_start(out=rb_col[:], in_=rb.rearrange("o (p t) -> (o p) t", t=PACK))
         for t in range(1, PACK):
             nc.sync.dma_start(out=x_rows[t][:], in_=xf_dealt[:, t, :])
         nc.sync.dma_start(g_list[:], offs2)
+        nc.sync.dma_start(out=pr_rows[0][:], in_=pr[0:P, :])
         for h in range(HALVES):
             nc.sync.dma_start(out=g_rows[h][:], in_=gt[h * P:(h + 1) * P, :])
+        nc.sync.dma_start(out=pr_rows[1][:], in_=pr[P:N, :])
         nc.sync.dma_start(out=mom_rows[:], in_=mom.rearrange("(p t) n -> p t n", t=PACK))
         nc.sync.dma_start(out=old_rows[:], in_=old.rearrange("(p t) n -> p t n", t=PACK))
+
+        warm_in = keep.tile([P, 1], F32, name="warm_in")
+        warm_out = keep.tile([P, 1], F32, name="warm_out")
+        nc.vector.memset(warm_in[:], 1.0)
+        nc.scalar.activation(warm_out[:], warm_in[:], ACT.Abs_reciprocal_sqrt)
 
         ident = keep.tile([P, P], F32, name="ident")
         make_identity(nc, ident[:])
@@ -64,65 +71,78 @@ def tile_list_moment_centred_errors_momentum_pl_kernel(tc, xf, ra, gt, rb, pr, m
         y_codes = keep.tile([P, N], U32, name="y_codes", align_bytes=64)
         y_scales = keep.tile([P, N], U8, name="y_scales", align_bytes=64)
 
+        ra_spread = ra_col[:].unsqueeze(1).to_broadcast([P, P, PACK])
+        rb_spread = rb_col[:].unsqueeze(1).to_broadcast([P, P, PACK])
+
         def turn(bank, sources, first):
             for i in range(PACK):
                 nc.tensor.matmul(bank[:, i, :], lhsT=sources[i], rhs=ident[:], is_transpose=True,
                                  start=(first and i == 0), stop=(not first and i == PACK - 1))
 
-        def by_byte(name, picked, sign):
+        def deal(name, picked, sign, on_scalar):
             dealt = keep.tile([P, PACK, P], F32, name=name)
-            nc.gpsimd.tensor_scalar(out=dealt[:], in0=picked[:].rearrange("p (q i) -> p i q", i=PACK),
-                                    scalar1=sign, scalar2=0.0, op0=ALU.mult, op1=ALU.add)
+            dst = dealt[:].rearrange("p i (c e) -> p c i e", e=RUN)
+            src = picked[:].rearrange("p (c e i) -> p c i e", e=RUN, i=PACK)
+            if on_scalar:
+                nc.scalar.activation(dst, src, ACT.Copy, scale=sign)
+            else:
+                nc.gpsimd.tensor_scalar(out=dst, in0=src, scalar1=sign, scalar2=0.0, op0=ALU.mult, op1=ALU.add)
             return [dealt[:, i, :] for i in range(PACK)]
 
-        def weigh_and_quantise(name, bank, weights, codes, scales):
-            rounded = keep.tile([P, P, PACK], BF16, name=name, align_bytes=64)
-            nc.vector.scalar_tensor_tensor(out=rounded[:], in0=bank[:].rearrange("p i c -> p c i"), scalar=-1.0,
-                                           in1=weights[:].unsqueeze(1).to_broadcast([P, P, PACK]),
-                                           op0=ALU.mult, op1=ALU.mult)
-            nc.vector.quantize_mx(out=codes.bitcast(E5M2), scales=scales, in_=rounded[:].rearrange("p c i -> p (c i)"))
-
         u_rounded = keep.tile([P, K, PACK], BF16, name="u_rounded", align_bytes=64)
+        g_rounded = keep.tile([P, N, PACK], BF16, name="g_rounded", align_bytes=64)
 
-        def features(t):
+        def centre(t):
             picked = keep.tile([P, J], F32, name="x_picked%d" % t)
             nc.scalar.activation(picked[:], x_rows[t][:].indirect(x_list[:]), ACT.Copy)
-            dealt = by_byte("x_dealt%d" % t, picked, 1.0)
+            dealt = deal("x_dealt%d" % t, picked, 1.0, False)
             sums = keep.tile([P, J // GROUP], F32, name="sums%d" % t)
             nc.vector.tensor_reduce(out=sums[:], in_=picked[:].rearrange("p (b e) -> p b e", e=GROUP),
                                     axis=mybir.AxisListType.X, op=ALU.add)
             neg_mean = keep.tile([P, J // GROUP, 2], F32, name="neg_mean%d" % t)
             nc.gpsimd.tensor_scalar(out=neg_mean[:], in0=sums[:].unsqueeze(2).to_broadcast([P, J // GROUP, 2]),
                                     scalar1=-1.0 / GROUP, scalar2=0.0, op0=ALU.mult, op1=ALU.add)
-            bank = psum.tile([P, PACK, P], F32, name="x_turned", bufs=3)
+            bank = psum.tile([P, PACK, P], F32, name="x_turned%d" % t, tag="turned", bufs=3)
             turn(bank, dealt, True)
             turn(bank, [neg_mean[:].rearrange("p b e -> p (b e)")] * PACK, False)
-            cols = slice(t * P, (t + 1) * P)
-            nc.vector.tensor_tensor(out=u_rounded[:, cols, :], in0=bank[:].rearrange("p i c -> p c i"),
-                                    in1=ra_col[:].unsqueeze(1).to_broadcast([P, P, PACK]), op=ALU.mult)
-            if t % 4 == 3:
-                both = slice((t - 3) * P, (t + 1) * P)
-                nc.vector.quantize_mx(out=u_codes[:, both].bitcast(E5M2), scales=u_scales[:, both],
-                                      in_=u_rounded[:, both, :].rearrange("p c i -> p (c i)"))
+            return bank
 
-        features(0)
-        g_banks = []
-        for h in range(HALVES):
-            bank = psum.tile([P, PACK, P], F32, name="g_turned%d" % h)
-            pr_view = pr_rows[:, h, :].rearrange("p (q i) -> p i q", i=PACK)
+        def errors(h):
+            bank = psum.tile([P, PACK, P], F32, name="g_turned%d" % h, tag="turned", bufs=3)
+            pr_view = pr_rows[h][:].rearrange("p (q i) -> p i q", i=PACK)
             turn(bank, [pr_view[:, i, :] for i in range(PACK)], True)
-            g_banks.append(bank)
+            picked = keep.tile([P, J], F32, name="g_picked%d" % h)
+            nc.scalar.activation(picked[:], g_rows[h][:].indirect(g_list[:]), ACT.Copy)
+            turn(bank, deal("g_dealt%d" % h, picked, -1.0, h == HALVES - 1), False)
+            return bank
+
+        def weigh_features(t, bank):
+            nc.vector.tensor_tensor(out=u_rounded[:, t * P:(t + 1) * P, :], in0=bank[:].rearrange("p i c -> p c i"),
+                                    in1=ra_spread, op=ALU.mult)
+
+        def weigh_errors(h, bank):
+            nc.vector.scalar_tensor_tensor(out=g_rounded[:, h * P:(h + 1) * P, :], in0=bank[:].rearrange("p i c -> p c i"),
+                                           scalar=-1.0, in1=rb_spread, op0=ALU.mult, op1=ALU.mult)
+
+        def quantise(codes, scales, rounded, cols):
+            nc.vector.quantize_mx(out=codes[:, cols].bitcast(E5M2), scales=scales[:, cols],
+                                  in_=rounded[:, cols, :].rearrange("p c i -> p (c i)"))
+
+        x_banks = [centre(0)]
         for t in range(1, PACK):
-            features(t)
+            x_banks.append(centre(t))
+            weigh_features(t - 1, x_banks[t - 1])
+        g_bank = errors(0)
+        weigh_errors(0, g_bank)
+        weigh_features(PACK - 1, x_banks[PACK - 1])
+        quantise(g_codes, g_scales, g_rounded, slice(0, P))
+        quantise(u_codes, u_scales, u_rounded, slice(0, K))
+        g_bank = errors(1)
+        weigh_errors(1, g_bank)
+        quantise(g_codes, g_scales, g_rounded, slice(P, N))
 
         y_out = out_0.rearrange("(p t) n -> p t n", t=PACK)
         words_out = out_1.rearrange("z p c r -> (z p) (c r)").bitcast(I32)
-        for h in range(HALVES):
-            cols = slice(h * P, (h + 1) * P)
-            picked = keep.tile([P, J], F32, name="g_picked%d" % h)
-            nc.scalar.activation(picked[:], g_rows[h][:].indirect(g_list[:]), ACT.Copy)
-            turn(g_banks[h], by_byte("g_dealt%d" % h, picked, -1.0), False)
-            weigh_and_quantise("g_rounded%d" % h, g_banks[h], rb_col, g_codes[:, cols], g_scales[:, cols])
 
         for h in range(HALVES):
             cols = slice(h * P, (h + 1) * P)
@@ -150,7 +170,9 @@ def tile_list_moment_centred_errors_momentum_pl_kernel(tc, xf, ra, gt, rb, pr, m
                 nc.vector.scalar_tensor_tensor(out=y[:, :, part], in0=old_rows[:, :, ns], scalar=0.5, in1=soft[:],
                                                op0=ALU.mult, op1=ALU.subtract)
                 y_rounded = keep.tile([P, CHUNK, PACK], BF16, name="y_rounded%d" % n0, align_bytes=64)
-                (nc.scalar.copy if c0 == 0 else nc.vector.tensor_copy)(out=y_rounded[:], in_=y[:, :, part].rearrange("p t c -> p c t"))
+                (nc.scalar.copy if c0 == 0 else nc.vector.tensor_copy)(
+                    out=y_rounded[:].rearrange("p (c e) t -> p c t e", e=RUN),
+                    in_=y[:, :, part].rearrange("p t (c e) -> p c t e", e=RUN))
                 nc.vector.quantize_mx(out=y_codes[:, ns].bitcast(E4M3), scales=y_scales[:, ns],
                                       in_=y_rounded[:].rearrange("p c t -> p (c t)"))
             nc.sync.dma_start(out=y_out[:, :, cols], in_=y[:])

from contextlib import ExitStack

import concourse.mybir as mybir
from concourse.masks import make_identity

K, J, N, T, V = 512, 512, 256, 1024, 1024
FLOPS = 2 * K * J * N

F32 = mybir.dt.float32
BF16 = mybir.dt.bfloat16
U32 = mybir.dt.uint32
I32 = mybir.dt.int32
U16 = mybir.dt.uint16
U8 = mybir.dt.uint8
E5M2 = mybir.dt.float8_e5m2_x4
E4M3 = mybir.dt.float8_e4m3fn_x4
ALU = mybir.AluOpType
ACT = mybir.ActivationFunctionType

P = 128
PACK = 4
GROUP = 8
HALVES = N // P
CHUNK = 64
RUN = 4


def tile_list_moment_centred_errors_momentum_pl_kernel(tc, xf, ra, gt, rb, pr, mom, old, offs, offs2, out_0, out_1, out_2):
    nc = tc.nc
    with ExitStack() as ctx:
        keep = ctx.enter_context(tc.tile_pool(name="keep", bufs=1))
        psum = ctx.enter_context(tc.psum_pool(name="psum", bufs=1))

        x_list = keep.tile([P, J // 16], U16, name="x_list")
        g_list = keep.tile([P, J // 16], U16, name="g_list")
        x_rows = [keep.tile([P, T], F32, name="x_rows%d" % t) for t in range(PACK)]
        g_rows = [keep.tile([P, V], F32, name="g_rows%d" % h) for h in range(HALVES)]
        pr_rows = [keep.tile([P, J], F32, name="pr_rows%d" % h) for h in range(HALVES)]
        mom_rows = keep.tile([P, PACK, N], F32, name="mom_rows")
        old_rows = keep.tile([P, PACK, N], F32, name="old_rows")
        ra_col = keep.tile([P, PACK], F32, name="ra_col")
        rb_col = keep.tile([P, PACK], F32, name="rb_col", tag="rb_then_step")
        nc.scalar.dma_start(out=ra_col[:], in_=ra.rearrange("o (p t) -> (o p) t", t=PACK))
        nc.scalar.dma_start(out=rb_col[:], in_=rb.rearrange("o (p t) -> (o p) t", t=PACK))

        xf_dealt = xf.rearrange("(p t) c -> p t c", t=PACK)
        nc.sync.dma_start(out=x_rows[0][:], in_=xf_dealt[:, 0, :])
        nc.sync.dma_start(x_list[:], offs)
        for t in range(1, PACK):
            nc.sync.dma_start(out=x_rows[t][:], in_=xf_dealt[:, t, :])
        nc.sync.dma_start(g_list[:], offs2)
        nc.sync.dma_start(out=pr_rows[0][:], in_=pr[0:P, :])
        for h in range(HALVES):
            nc.sync.dma_start(out=g_rows[h][:], in_=gt[h * P:(h + 1) * P, :])
        nc.sync.dma_start(out=pr_rows[1][:], in_=pr[P:N, :])
        nc.sync.dma_start(out=mom_rows[:], in_=mom.rearrange("(p t) n -> p t n", t=PACK))
        nc.sync.dma_start(out=old_rows[:], in_=old.rearrange("(p t) n -> p t n", t=PACK))

        warm_in = keep.tile([P, 1], F32, name="warm_in")
        warm_out = keep.tile([P, 1], F32, name="warm_out")
        nc.vector.memset(warm_in[:], 1.0)
        nc.scalar.activation(warm_out[:], warm_in[:], ACT.Abs_reciprocal_sqrt)

        ident = keep.tile([P, P], F32, name="ident")
        make_identity(nc, ident[:])

        u_codes = keep.tile([P, K], U32, name="u_codes", align_bytes=64)
        u_scales = keep.tile([P, K], U8, name="u_scales", align_bytes=64)
        g_codes = keep.tile([P, N], U32, name="g_codes", align_bytes=64)
        g_scales = keep.tile([P, N], U8, name="g_scales", align_bytes=64)
        y_codes = keep.tile([P, N], U32, name="y_codes", align_bytes=64)
        y_scales = keep.tile([P, N], U8, name="y_scales", align_bytes=64)

        ra_spread = ra_col[:].unsqueeze(1).to_broadcast([P, P, PACK])
        rb_spread = rb_col[:].unsqueeze(1).to_broadcast([P, P, PACK])

        def turn(bank, sources, first):
            for i in range(PACK):
                nc.tensor.matmul(bank[:, i, :], lhsT=sources[i], rhs=ident[:], is_transpose=True,
                                 start=(first and i == 0), stop=(not first and i == PACK - 1))

        def deal(name, picked, sign, on_scalar):
            dealt = keep.tile([P, PACK, P], F32, name=name)
            dst = dealt[:].rearrange("p i (c e) -> p c i e", e=RUN)
            src = picked[:].rearrange("p (c e i) -> p c i e", e=RUN, i=PACK)
            if on_scalar:
                nc.scalar.activation(dst, src, ACT.Copy, scale=sign)
            else:
                nc.gpsimd.tensor_scalar(out=dst, in0=src, scalar1=sign, scalar2=0.0, op0=ALU.mult, op1=ALU.add)
            return [dealt[:, i, :] for i in range(PACK)]

        u_rounded = keep.tile([P, K, PACK], BF16, name="u_rounded", align_bytes=64)
        g_rounded = keep.tile([P, N, PACK], BF16, name="g_rounded", align_bytes=64)

        def centre(t):
            picked = keep.tile([P, J], F32, name="x_picked%d" % t)
            nc.scalar.activation(picked[:], x_rows[t][:].indirect(x_list[:]), ACT.Copy)
            dealt = deal("x_dealt%d" % t, picked, 1.0, False)
            sums = keep.tile([P, J // GROUP], F32, name="sums%d" % t)
            nc.vector.tensor_reduce(out=sums[:], in_=picked[:].rearrange("p (b e) -> p b e", e=GROUP),
                                    axis=mybir.AxisListType.X, op=ALU.add)
            neg_mean = keep.tile([P, J // GROUP, 2], F32, name="neg_mean%d" % t)
            nc.gpsimd.tensor_scalar(out=neg_mean[:], in0=sums[:].unsqueeze(2).to_broadcast([P, J // GROUP, 2]),
                                    scalar1=-1.0 / GROUP, scalar2=0.0, op0=ALU.mult, op1=ALU.add)
            bank = psum.tile([P, PACK, P], F32, name="x_turned%d" % t, tag="turned", bufs=3)
            turn(bank, dealt, True)
            turn(bank, [neg_mean[:].rearrange("p b e -> p (b e)")] * PACK, False)
            return bank

        def errors(h):
            bank = psum.tile([P, PACK, P], F32, name="g_turned%d" % h, tag="turned", bufs=3)
            pr_view = pr_rows[h][:].rearrange("p (q i) -> p i q", i=PACK)
            turn(bank, [pr_view[:, i, :] for i in range(PACK)], True)
            picked = keep.tile([P, J], F32, name="g_picked%d" % h)
            nc.scalar.activation(picked[:], g_rows[h][:].indirect(g_list[:]), ACT.Copy)
            turn(bank, deal("g_dealt%d" % h, picked, -1.0, h == HALVES - 1), False)
            return bank

        def weigh_features(t, bank):
            nc.vector.tensor_tensor(out=u_rounded[:, t * P:(t + 1) * P, :], in0=bank[:].rearrange("p i c -> p c i"),
                                    in1=ra_spread, op=ALU.mult)

        def weigh_errors(h, bank):
            nc.vector.scalar_tensor_tensor(out=g_rounded[:, h * P:(h + 1) * P, :], in0=bank[:].rearrange("p i c -> p c i"),
                                           scalar=-1.0, in1=rb_spread, op0=ALU.mult, op1=ALU.mult)

        def quantise(codes, scales, rounded, cols):
            nc.vector.quantize_mx(out=codes[:, cols].bitcast(E5M2), scales=scales[:, cols],
                                  in_=rounded[:, cols, :].rearrange("p c i -> p (c i)"))

        x_banks = [centre(0)]
        for t in range(1, PACK):
            x_banks.append(centre(t))
            weigh_features(t - 1, x_banks[t - 1])
        g_bank = errors(0)
        weigh_errors(0, g_bank)
        weigh_features(PACK - 1, x_banks[PACK - 1])
        quantise(g_codes, g_scales, g_rounded, slice(0, P))
        quantise(u_codes, u_scales, u_rounded, slice(0, K))
        g_bank = errors(1)
        weigh_errors(1, g_bank)
        quantise(g_codes, g_scales, g_rounded, slice(P, N))

        y_out = out_0.rearrange("(p t) n -> p t n", t=PACK)
        words_out = out_1.rearrange("z p c r -> (z p) (c r)").bitcast(I32)

        for h in range(HALVES):
            cols = slice(h * P, (h + 1) * P)
            moment = psum.tile([P, PACK, P], F32, name="moment%d" % h)
            for t in range(PACK):
                rows = slice(t * P, (t + 1) * P)
                nc.tensor.matmul_mx(out=moment[:, t, :], lhsT=u_codes[:, rows].bitcast(E5M2), lhsT_scale=u_scales[:, rows],
                                    rhs=g_codes[:, cols].bitcast(E5M2), rhs_scale=g_scales[:, cols], start=True, stop=True)
            y = keep.tile([P, PACK, P], F32, name="y%d" % h)
            for c0 in range(0, P, CHUNK):
                n0 = h * P + c0
                part = slice(c0, c0 + CHUNK)
                ns = slice(n0, n0 + CHUNK)
                step = keep.tile([P, PACK, CHUNK], F32, name="step%d" % n0, tag="rb_then_step" if n0 == 0 else "step%d" % n0)
                nc.vector.scalar_tensor_tensor(out=step[:], in0=mom_rows[:, :, ns], scalar=15.0, in1=moment[:, :, part],
                                               op0=ALU.mult, op1=ALU.add)
                size = keep.tile([P, PACK, CHUNK], F32, name="size%d" % n0)
                nc.scalar.activation(size[:], step[:], ACT.Abs)
                root = keep.tile([P, PACK, CHUNK], F32, name="root%d" % n0)
                nc.scalar.activation(root[:], size[:], ACT.Abs_reciprocal_sqrt, bias=25.0)
                inverse = keep.tile([P, PACK, CHUNK], F32, name="inverse%d" % n0)
                nc.scalar.activation(inverse[:], root[:], ACT.Square)
                soft = keep.tile([P, PACK, CHUNK], F32, name="soft%d" % n0)
                nc.vector.tensor_tensor(out=soft[:], in0=step[:], in1=inverse[:], op=ALU.mult)
                nc.vector.scalar_tensor_tensor(out=y[:, :, part], in0=old_rows[:, :, ns], scalar=0.5, in1=soft[:],
                                               op0=ALU.mult, op1=ALU.subtract)
                y_rounded = keep.tile([P, CHUNK, PACK], BF16, name="y_rounded%d" % n0, align_bytes=64)
                (nc.scalar.copy if c0 == 0 else nc.vector.tensor_copy)(
                    out=y_rounded[:].rearrange("p (c e) t -> p c t e", e=RUN),
                    in_=y[:, :, part].rearrange("p t (c e) -> p c t e", e=RUN))
                nc.vector.quantize_mx(out=y_codes[:, ns].bitcast(E4M3), scales=y_scales[:, ns],
                                      in_=y_rounded[:].rearrange("p c t -> p (c t)"))
            nc.sync.dma_start(out=y_out[:, :, cols], in_=y[:])
            nc.sync.dma_start(out=words_out[:, cols], in_=y_codes[:, cols].bitcast(I32))

        scales_out = out_2.rearrange("z q c -> (z q) c").bitcast(I32)
        for q in range(4):
            queue = nc.sync if q % 2 == 0 else nc.scalar
            queue.dma_start(out=scales_out[4 * q:4 * q + 4, :], in_=y_scales[32 * q:32 * q + 4, :].bitcast(I32))
